import numpy as np, ml_dtypes
CORES = [16,18,20,22]
N = 4
import mx_ref
BF = ml_dtypes.bfloat16
def gcols(t, e):
    v = np.concatenate([t.reshape(8, 16, -1, 4), np.zeros((8, 16, 1, 4), BF)], axis=2)
    return np.ascontiguousarray(np.stack([v[g][:, e[g]] for g in range(8)])).reshape(128, -1)
def tile(rs):
    return np.stack(rs, axis=2).reshape(128, -1).astype(BF)
def pick(q, e):
    c = np.concatenate([q[0].reshape(128, -1, 4), np.zeros((128, 1, 4), np.uint8)], axis=1); s = np.concatenate([q[1], np.ones((16, 1), np.uint8)], axis=1)
    return (np.ascontiguousarray(c[:, e].reshape(128, -1)), np.ascontiguousarray(s[:, e]))
def join(*qs):
    return (np.concatenate([q[0] for q in qs], axis=1), np.concatenate([q[1] for q in qs], axis=1))
def put(q, e, v):
    c, s = q[0].reshape(128, -1, 4).copy(), q[1].copy(); c[:, e] = v[0].reshape(128, -1, 4); s[:, e] = v[1]
    return (c.reshape(128, -1), s)
def pk(c, s):
    return (np.ascontiguousarray(c), mx_ref.live(s))
def emit(q):
    return q[0], q[1]
def packed(v, rng):
    q = [mx_ref.quantize(np.ascontiguousarray(v[r])) for r in range(N)]
    return np.stack([a for a, b in q]), np.stack([mx_ref.plane(b, rng) for a, b in q])
def values_of_codes():
    e, c = np.zeros((128, 128, 4), np.float32), np.zeros((128, 2, 4), np.uint8)
    e[np.arange(128), np.arange(128), 0] = 1
    c[:127, :, 0] = np.arange(256).reshape(2, 128).T[:127]
    return mx_ref.matmul(mx_ref.quantize(e.reshape(128, 512).astype(BF)), (c.reshape(128, 8), np.full((16, 2), 127, np.uint8))).T.reshape(-1).astype(np.float64)
CODE_VALUE, SCALE_VALUE = values_of_codes(), 2.0 ** (np.arange(256) - 127.0)
def decode(q):
    return (CODE_VALUE[q[0]].reshape(16, 8, -1, 4) * SCALE_VALUE[q[1]][:, None, :, None] + 0.0).reshape(128, -1).astype(np.float32)
def f(rng, *shape):
    return mx_ref.flush((rng.standard_normal(shape, dtype=np.float32) * np.exp2(rng.integers(-2, 3, shape[:-1] + (1,)))).astype(BF))
def wide(rng, *shape, cols=0):
    v = rng.standard_normal(shape, dtype=np.float32) * np.exp2(rng.integers(-12, 13, shape)).astype(np.float32)
    if cols: v *= np.repeat(np.exp2(rng.integers(-cols, cols + 1, shape[:-2] + (1, shape[-1] // 4))) * (rng.random(shape[:-2] + (1, shape[-1] // 4)) > 0.0625), 4, axis=-1).astype(np.float32)
    return mx_ref.flush(v.astype(BF))
C, P, R = 384, 96, 2
def big(v):
    v = v.astype(np.float32)
    v[np.abs(v) < np.float32(2.0 ** -16)] = 0
    return v.astype(BF)
def numbers_of(rng):
    return {"x": big(f(rng, N, 128, 4 * C)), "u": np.array(f(rng, N, 128, 512)), "v": np.array(f(rng, N, 128, 512))}
def layers(rng):
    return big(f(rng, N, 128, 2048)).reshape(N, 8, 16, 4, 8, 16, 4)
def weights(rng, w):
    c, p = packed(np.ascontiguousarray(w).reshape(N, 128, 2048), rng)
    return {"wc": c, "ws": p}
def setup_inputs(rng):
    return {**numbers_of(rng), **weights(rng, layers(rng))}
def setup_inputs_ties(rng):
    d = numbers_of(rng)
    e = rng.permutation(N)
    x = d["x"].reshape(N, 8, 16, C, 4)
    for r in range(N):
        k = rng.permutation(C) % 3
        if r == e[0]: k = np.zeros(C, int)
        elif r in e[2::2]: k = rng.permutation(3)[np.arange(C) % 3]
        a = x[r][:, :8, :3].copy()
        a[:, :, 2] = 0
        x[r][:, :8] = a[:, :, k]
    x[e[1]] = 0
    u = d["u"].reshape(N, 8, 16, 128, 4)
    for i in range(5): u[:, :, 8:, i::16] = 0
    w = layers(rng)
    w[:, :, :, :, :, :8] = 0
    return {"x": x.reshape(N, 128, 4 * C), "u": u.reshape(N, 128, 512), "v": d["v"], **weights(rng, w)}
def setup_inputs_near(rng):
    d = numbers_of(rng)
    x = d["x"].astype(np.float32).reshape(N, 8, 16, C, 4)
    x[:, :, :9] = 0
    u = d["u"].reshape(N, 128, 128, 4)
    for i in range(5): u[:, :, i::16] = 0
    o = rng.permutation(N) % 4
    for r in range(N):
        k = 2.0 ** -30 if o[r] else 1.0
        c = rng.integers(0, 2, (8, 1)) * 2.0 - 1.0
        s = rng.integers(-1, 2, (8, C, 4))
        if o[r] < 2:
            n = rng.integers(0, 16, (8, C))
            x[r, :, 0] = ((n[:, :, None] >> np.arange(4)) & 1) * np.exp2(np.arange(4) - 23.0)
            x[r, :, 1, :, 0] = 2.0 ** -10
            x[r, :, 2] = s * 2.0 ** -10
            x[r, :, 8, :, 0] = c
        else:
            x[r, :, 0, :, 0] = c * rng.integers(1, 16, (8, C)) * 2.0 ** -29
            x[r, :, 2] = s * 2.0 ** -29
        for g in rng.permutation(8)[:4]: x[r, g, 8 if o[r] < 2 else 0, rng.integers(C), 0] = 2.0 ** 29 * (rng.integers(0, 2) * 2.0 - 1.0)
        for h in range(0, 128, 16):
            u[r, h, h + 4] = k
            u[r, h + 1, h + 4, 0] = k
            u[r, h + 8, h + 4, 0] = k
            for i in range(4): u[r, h + 2, h + i, i] = k
    w = layers(rng)
    w[:, :, :9] = 0
    w[:, :, :, :, :, :9] = 0
    return {"x": x.reshape(N, 128, 4 * C).astype(BF), "u": u.reshape(N, 128, 512), "v": d["v"], **weights(rng, w)}
def setup_inputs_skew(rng):
    d = numbers_of(rng)
    x = d["x"].astype(np.float32).reshape(N, 8, 16, C, 4)
    t = (1 + (2 * rng.integers(0, 64, (N, 8, 8, C // 2, 4)) + 1) / 128) * np.exp2(-rng.integers(8, 15, (N, 8, 8, C // 2, 4)).astype(float)) * (rng.integers(0, 2, (N, 8, 8, C // 2, 4)) * 2.0 - 1.0)
    t[:, :, 3, :, 1] = 1.96875
    x[:, :, 8:, ::2] = t * np.exp2(rng.integers(-2, 3, (N, 8, 1, C // 2, 1)).astype(float))
    u = d["u"].reshape(N, 128, 128, 4)
    for i in range(5): u[:, :, i::16] = 0
    for h in range(0, 128, 16):
        for b in range(12): u[:, h + b // 4, h + 4, b % 4] = 2.0 ** b
        for i in range(4): u[:, h + 3, h + i, i] = 1
    n = -(-C // 7)
    n2 = n - (-(C - n) // 5)
    n3 = n2 - (-(C - n2) // 3)
    down = C - 1 - np.arange(C)
    for r in range(N):
        for j, g in enumerate(rng.permutation(8)):
            a = np.append(rng.permutation(np.delete(np.arange(4), j % 4)), j % 4)
            two = np.zeros((C, 4), int)
            if j < 6:
                two[:n, a[0]] = 1
                two[n:n2, a[1]] = 1
            if j < 4: two[n2:n3, a[2]] = 1
            if j >= 6: two[-(-2 * C // 5):] = 1
            o = rng.permutation(C)
            x[r, g][:3, o] = (down[None, :, None] >> (4 * np.arange(3)[:, None, None] + np.arange(4))) & 1
            x[r, g][3, o] = np.where(two > 0, 1, -rng.integers(0, 2, (C, 4)))
    w = layers(rng)
    w[:, :, :, :, :, :4] = 0
    return {"x": x.reshape(N, 128, 4 * C).astype(BF), "u": u.reshape(N, 128, 512), "v": d["v"], **weights(rng, w)}
def setup_inputs_huge(rng):
    d = numbers_of(rng)
    o = rng.permutation(N)
    h = rng.permutation(8)
    x = -0.95 - 0.05 * rng.random((N, 8, 16, C, 4))
    x[:, h[4:]] = (0.75 + 0.1 * rng.random((N, 4, 16, C, 4))) * rng.choice([-1.0, 1.0], (N, 4, 1, C, 1))
    u = d["u"].reshape(N, 128, 128, 4)
    for i in range(5): u[:, :, i::16] = 0
    for r in range(N):
        if o[r] < N // 2: x[r] = (0.8 + 0.1 * rng.random((8, 16, C, 4))) * rng.choice([-1.0, 1.0], (1, 1, C, 1))
        for g in range(8):
            for i in range(5):
                a, n = 16 * int(rng.choice(h[4:])), 16
                if i == 4 and o[r] < N // 2: a, n = 0, 128
                u[r, a:a + n, 16 * g + i] = (2.0 ** 30 * (1 - 0.05 * rng.random((n, 4))) * rng.choice([-1.0, 1.0])).astype(np.float32).astype(BF)
    w = np.zeros((N, 128, 4, 128, 4), np.float32)
    i = np.arange(128)
    for b in range(4): w[:, i, b, i, b] = -1
    return {"x": (2.0 ** 30 * x).astype(np.float32).reshape(N, 128, 4 * C).astype(BF), "u": u.reshape(N, 128, 512), "v": d["v"], **weights(rng, w.astype(BF))}
def setup_inputs_spread(rng):
    d = setup_inputs(rng)
    d["x"] = big(wide(rng, N, 128, 4 * C, cols=6))
    return d
def check_inputs(d):
    b = []
    for k in ("x", "u", "v"):
        a = np.abs(d[k].astype(np.float32))
        if not (np.isfinite(a).all() and ((a == 0) | (a >= 2.0 ** -30) & (a <= 2.0 ** 30)).all()): b.append("a value of " + k)
    none, least, most = [emit(mx_ref.quantize(np.full((128, 16), k, np.float32).astype(BF)))[1][0, 0] for k in (0.0, 2.0 ** -30, 2.0 ** 30)]
    for r in range(N):
        if ((d["wc"][r] == 0x7F) | (d["wc"][r] == 0xFF)).any(): b.append("wc: a code that is no number")
        s = mx_ref.live(d["ws"][r])
        if ((s != none) & ((s < least) | (s > most))).any(): b.append("ws: a scale out of range")
    return b
def divide(sums):
    g = np.arange(8)
    first, end = np.zeros((4, 8), np.int64), np.full((4, 8), C)
    a, left = np.zeros(8, np.int64), np.ones((4, 8), bool)
    for m in (4, 3, 2):
        worth = sums - np.stack([sums[k, g, a] for k in range(4)])[:, :, None]
        e = np.sum(m * worth < worth[:, :, -1:], axis=2)
        e[~left] = C + 1
        k = np.argmin(e, axis=0)
        first[k, g] = a
        a = e[k, g]
        end[k, g] = a
        left[k, g] = False
    first[np.argmax(left, axis=0), g] = a
    return first, end
def reference(x, u, v, wc, ws):
    qu = [mx_ref.quantize(u[r]) for r in range(N)]
    lay = [pk(wc[r], ws[r]) for r in range(N)]
    now = [x[r] for r in range(N)]
    of = [np.arange(k * P, k * P + P) for k in range(4)]
    slot_of = np.zeros((N, 8, C), np.int64)
    for t in range(R):
        sent, best, made = [], [], []
        slot_of[:] = -1
        for r in range(N):
            s = mx_ref.matmul(qu[r], mx_ref.quantize(now[r])) + np.float32(0.0)
            o = np.argsort(-s[4::16], axis=1, kind="stable")
            worth = np.stack([1 + (np.take_along_axis(s[k::16], o, axis=1) > 0) for k in range(4)])
            first, end = divide(np.concatenate([np.zeros((4, 8, 1), np.int64), np.cumsum(worth, axis=2)], axis=2))
            slots = []
            for k in range(4):
                i = first[k][:, None] + np.arange(P)
                slots.append(np.where(i < end[k][:, None], np.take_along_axis(o, np.minimum(i, C - 1), axis=1), -1))
            slots = np.concatenate(slots, axis=1)
            for g in range(8):
                j = np.nonzero(slots[g] >= 0)[0]
                slot_of[r, g, slots[g, j]] = j
            sent.append(mx_ref.quantize(gcols(now[r], slots)))
            best.append(gcols(now[r], o[:, :P]))
        for r in range(N):
            came = decode(join(*[pick(sent[(r - k) % N], of[k]) for k in range(4)]))
            z = mx_ref.quantize(((came + np.tile(best[r].astype(np.float32), (1, 4))) * np.float32(0.5)).astype(BF))
            made.append(mx_ref.quantize(tile([mx_ref.matmul(pick(lay[r], np.arange(128 * b, 128 * b + 128)), z) * np.float32(0.03125) for b in range(4)])))
        for r in range(N):
            back = decode(join(*[pick(made[(r + k) % N], of[k]) for k in range(4)])).astype(BF)
            now[r] = (now[r].astype(np.float32) + gcols(back, slot_of[r]).astype(np.float32)).astype(BF)
    y, sl = np.zeros((N, 128, C), np.float32), np.zeros((N, 8, C), np.float32)
    oc, osc = np.zeros((N, 128, 4 * C), np.uint8), np.zeros((N, 16, C), np.uint8)
    for r in range(N):
        q = mx_ref.quantize(now[r])
        y[r] = mx_ref.matmul(mx_ref.quantize(v[r]), q)
        sl[r] = slot_of[r]
        oc[r], osc[r] = emit(q)
    return {"y": y, "sl": sl, "oc": oc, "osc": osc}

from concourse.bass import DstId, RemoteDMATransfer
from concourse.mybir import dt, AluOpType as ALU, AxisListType, ActivationFunctionType as ACT

C, P = 384, 96
R3 = 3 * P
HALF = R3 // 2
BIG = 1.0e28
DUMP = 480
POS = DUMP * 5
NB0 = 1024
XW = NB0 + C

SCRATCH = {}
SEMAPHORES = ["sv", "ss", "st", "sp"]
WIDTH = {}
HOME = {}


def _b(name, n, dtype="float32", where="sbuf"):
    SCRATCH[name] = (where, [128, n], dtype)
    WIDTH[name] = n
    HOME[name] = (name, 0)


def _q(name, n):
    _b("q" + name, n, "float8_e4m3fn_x4")
    _b("s" + name, n, "uint8")


def _pack(buf, pieces):
    at = 0
    for name, n in pieces:
        WIDTH[name] = n
        HOME[name] = (buf, at)
        at += -(-n // 8) * 8
    SCRATCH[buf] = ("sbuf", [128, at], "float32")


for _i in range(8):
    _b("ps%d" % _i, 512, "float32", "psum")
for _r in range(2):
    _b("xw%d" % _r, 4 * XW, "bfloat16")
    _b("srt%d" % _r, POS)
    for _n, _w in (("x", C), ("b", C), ("lb", R3), ("h", R3), ("lh", R3)):
        _q("%s%d" % (_n, _r), _w)
    SEMAPHORES += ["ab%d" % _r, "ah%d" % _r, "lb%d" % _r, "lh%d" % _r]
_b("xf", 4 * C, "bfloat16")
for _n, _w in (("xf", C), ("u", 128), ("ua", 128), ("v", 128), ("w", 512), ("e1", 512), ("eh", 512), ("g", 128), ("z0", 128), ("z", R3), ("h0k", 128)):
    _q(_n, _w)
for _n, _w in (("ut", 512), ("vt", 512), ("eone", 2048), ("ebt", 2048), ("ebth", 2048), ("gt", 512), ("gt1", 512), ("bt", 4 * C),
               ("e3", 4 * R3), ("zt0", 512), ("zt", 4 * R3), ("ht0", 512), ("ht", 4 * R3), ("jk", 4416), ("fs", C), ("fb", C), ("rz16", C), ("cm", 160)):
    _b(_n, _w, "bfloat16")
MTN = (384, 320, 256, 192, 128, 128)
for _i in range(6):
    _b("mt%d" % _i, 4 * MTN[_i], "bfloat16")
    _q("m%d" % _i, MTN[_i])
_b("wsc", 392)
_b("yt", C)
_pack("consts", [(_n, C) for _n in ("r16", "r4", "ij", "rs1", "nm1", "nm2", "rs4", "n41", "n42", "nm16", "rst16", "nm4", "rst4", "ioj", "ni")]
      + [(_n, 24) for _n in ("c24", "ct", "ki", "si", "st", "koff")] + [("cols", 16), ("hm", 32), ("hm1", 32), ("msk", 40), ("rc", 8)])
_pack("wide", [(_n, C) for _n in ("vm", "zz", "dg", "cx", "z2", "rl", "fj", "gm", "zs", "gm2", "zs2", "slg", "sl1", "sl2")] + [("ge", P), ("ze", P)])
_pack("small", [(_n, 24) for _n in ("rsum", "cd", "pd", "pf")] + [("ky", 40), ("kt", 32), ("wa", 48), ("tmp", 24 * 16)]
      + [(_n, 8) for _n in ("kk", "cnt", "th", "rm", "rr", "aa", "a8", "am", "w3", "w4")])
for _n, _w in (("icol", 16), ("ilist", 8)):
    _b(_n, _w, "int32")
for _n, _w in (("ulist", 8), ("pl", 24), ("of", 8), ("pu", 24), ("l1", 96), ("l2", 96), ("l3", 24)):
    _b(_n, _w, "uint16")
NDMA = 24
SEMAPHORES += ["d%d" % _i for _i in range(NDMA)]


def rank_program(g, core, T, topo):
    rank = T.rank_of(core)
    if rank is None:
        return
    V, S, PE, G, SY = "v", "s", "t", "p", "y"
    eng = {V: g.vector, S: g.scalar, PE: g.tensor, G: g, SY: g.sync}
    count = {V: 0, S: 0, PE: 0, G: 0}
    clock = {q: {} for q in eng}
    evclock = {}
    hist = {}
    used = []

    def A(n, lo=None, hi=None, st=1):
        if lo is None:
            lo, hi = 0, WIDTH[n]
        buf, at = HOME[n]
        lo, hi = lo + at, hi + at
        return (T[buf][:, lo:hi] if st == 1 else T[buf][:, lo:hi:st], (buf, lo, hi, st))

    def meet(a, b):
        if a[0].startswith("ps"):
            return True
        if a[2] <= b[1] or b[2] <= a[1]:
            return False
        if a[3] == b[3] and a[3] > 1 and (a[1] - b[1]) % a[3]:
            return False
        return True

    def need(q, outs, ins):
        want = {}
        for kind, regs in (("w", outs), ("r", ins)):
            for r in regs:
                for (r2, k2, ev) in hist.get(r[0], ()):
                    bank = r[0].startswith("ps") and ev[2] != q
                    if (kind == "w" or k2 == "w" or bank) and meet(r, r2):
                        want[ev[0]] = max(want.get(ev[0], 0), ev[1])
        ck = clock[q]
        for s in sorted(want):
            n = want[s]
            if ck.get(s, 0) >= n:
                continue
            eng[q].wait_ge(T.sem[s], n)
            ck[s] = n
            for s2, n2 in evclock.get((s, n), {}).items():
                ck[s2] = max(ck.get(s2, 0), n2)

    def note(outs, ins, ev):
        for r in outs:
            h = hist.setdefault(r[0], [])
            if r[3] == 1:
                h[:] = [e for e in h if not (e[0][1] >= r[1] and e[0][2] <= r[2])]
            h.append((r, "w", ev))
        for r in ins:
            hist.setdefault(r[0], []).append((r, "r", ev))

    def op(q, fn, outs, ins):
        need(q, outs, ins)
        count[q] += 1
        s = "s" + q
        fn(eng[q]).then_inc(T.sem[s], 1)
        evclock[(s, count[q])] = dict(clock[q])
        note(outs, ins, (s, count[q], q))

    def dma(q, out, in_, outs, ins):
        need(q, outs, ins)
        s = "d%d" % len(used)
        used.append(s)
        eng[q].dma_start(out, in_).then_inc(T.sem[s], 16)
        evclock[(s, 16)] = dict(clock[q])
        note(outs, ins, (s, 16, s))

    def sc(x):
        return (x[0], [x[1]]) if isinstance(x, tuple) else (x, [])

    def ts(o, i, s1, s2, op0, op1=None):
        a, ra = sc(s1)
        b, rb = sc(s2)
        if op1 is None:
            op(V, lambda e: e.tensor_scalar(o[0], i[0], a, None, op0), [o[1]], [i[1]] + ra)
        else:
            op(V, lambda e: e.tensor_scalar(o[0], i[0], a, b, op0, op1), [o[1]], [i[1]] + ra + rb)

    def tt(o, i, j, o_):
        op(V, lambda e: e.tensor_tensor(o[0], i[0], j[0], o_), [o[1]], [i[1], j[1]])

    def scan(o, i, j, a, b):
        op(V, lambda e: e.tensor_tensor_scan(o[0], i[0], j[0], 0.0, a, b), [o[1]], [i[1], j[1]])

    def red(o, i, o_):
        op(V, lambda e: e.tensor_reduce(o[0], i[0], AxisListType.X, o_), [o[1]], [i[1]])

    def cp(o, i):
        op(V, lambda e: e.tensor_copy(o[0], i[0]), [o[1]], [i[1]])

    def ms(o, c):
        op(V, lambda e: e.memset(o[0], c), [o[1]], [])

    def act(o, i, f, scale=1.0, bias=None, acc=None):
        if acc is not None:
            op(S, lambda e: e.activation(o[0], i[0], f, accum_out=acc[0]), [o[1], acc[1]], [i[1]])
        elif bias is None:
            op(S, lambda e: e.activation(o[0], i[0], f, scale=scale), [o[1]], [i[1]])
        else:
            b, rb = sc(bias)
            op(S, lambda e: e.activation(o[0], i[0], f, bias=b, scale=scale), [o[1]], [i[1]] + rb)

    def pick(q, o, w, l, scale=1.0):
        x = w[0].indirect(l[0])
        if q == V:
            op(V, lambda e: e.tensor_copy(o[0], x), [o[1]], [w[1], l[1]])
        else:
            op(S, lambda e: e.activation(o[0], x, ACT.Copy, scale=scale), [o[1]], [w[1], l[1]])

    def picktt(o, w, l, j, o_):
        x = w[0].indirect(l[0])
        op(V, lambda e: e.tensor_tensor(o[0], x, j[0], o_), [o[1]], [w[1], l[1], j[1]])

    def put(w, l, i):
        x = w[0].indirect(l[0])
        op(V, lambda e: e.tensor_copy(x, i[0]), [w[1]], [l[1], i[1]])

    def quant(n, lo, hi, i):
        o, s = A("q" + n, lo, hi), A("s" + n, lo, hi)
        op(V, lambda e: e.quantize_mx(o[0], s[0], i[0]), [o[1], s[1]], [i[1]])

    def mm(bank, n, ln, llo, rn, rlo, start=True, stop=True):
        o = A("ps%d" % bank, 0, n)
        l, ls = A("q" + ln, llo, llo + 128), A("s" + ln, llo, llo + 128)
        r, rs = A("q" + rn, rlo, rlo + n), A("s" + rn, rlo, rlo + n)
        ins = [l[1], ls[1], r[1], rs[1]]
        op(PE, lambda e: e.matmul_mx(o[0], l[0], ls[0], r[0], rs[0], start, stop), [o[1]] if start else [], ins)
        if not start:
            note([o[1]], [], ("st", count[PE], PE))

    def iota(o, pattern, base, cm):
        op(G, lambda e: e.iota(o[0], pattern, base, cm, allow_small_or_imprecise_dtypes=True), [o[1]], [])

    def asel(o, i, pattern, cmp, base, cm):
        op(G, lambda e: e.affine_select(o[0], i[0], pattern, cmp, 0.0, base, cm), [o[1]], [i[1]])

    def load(q, name, lo, hi, src):
        a = A(name, lo, hi)
        dma(q, a[0], src, [a[1]], [])

    load(SY, "xw0", 0, 4 * C, T.x[:])
    load(S, "ut", 0, 512, T.u[:])
    load(SY, "xw0", 2048, 2048 + 4 * C, T.x[:])
    wq = A("qw")
    dma(SY, wq[0].bitcast(dt.uint8), T.wc[:], [wq[1]], [])
    load(SY, "sw", 0, 512, T.ws[:])
    load(SY, "vt", 0, 512, T.v[:])

    icol = lambda k: A("icol", k, k + 1)
    col = lambda k: A("cols", k, k + 1)
    op(G, lambda e: e.iota(icol(0)[0], [[1, 1]], 0, 1), [icol(0)[1]], [])
    iota(A("r16"), [[0, 24], [1, 16]], 0, 0)
    op(G, lambda e: e.iota(A("ilist")[0], [[16, 8]], 4, 0), [A("ilist")[1]], [])
    iota(A("ct"), [[-16, 24]], 368, 0)
    iota(A("ki"), [[1, 4], [0, 6]], 0, 0)
    iota(A("st"), [[0, 4], [16, 6]], -C, 0)
    iota(A("koff"), [[DUMP, 4], [0, 6]], DUMP, 0)
    iota(A("hm"), [[1, 2], [0, 16]], 0, 0)
    iota(A("ij"), [[1, C]], 0, 0)
    ms(A("eone"), 1.0)
    asel(A("gt1"), A("eone", 0, 512), [[-16, 8], [0, 64]], ALU.is_ge, 0, 1)
    asel(A("gt"), A("gt1"), [[16, 8], [0, 64]], ALU.is_ge, 15, -1)
    iota(A("r4"), [[0, 96], [1, 4]], 0, 0)
    asel(A("ebt"), A("eone"), [[1000, 4], [-1, 128], [-1000, 4]], ALU.is_equal, 0, 1)
    iota(A("xw0", 3584, 4096), [[0, 512]], 0, 0)
    iota(A("xw1", 1536, 2048), [[0, 512]], 0, 0)
    iota(A("xw1", 3584, 4096), [[0, 512]], 0, 0)
    iota(A("zt0", 384, 512), [[0, 128]], 0, 0)
    iota(A("ht0", 384, 512), [[0, 128]], 0, 0)

    ts(icol(1), icol(0), 15, None, ALU.bitwise_and)
    ts(icol(2), icol(0), 3, None, ALU.bitwise_and)
    ts(icol(3), icol(0), 2, 3, ALU.logical_shift_right, ALU.bitwise_and)
    ts(icol(4), icol(0), 4, 1, ALU.logical_shift_right, ALU.bitwise_and)
    cp(A("cols", 1, 5), A("icol", 1, 5))
    ts(col(5), col(1), -1.0, None, ALU.mult)
    ts(col(6), col(3), -1.0, None, ALU.mult)
    act(A("nm1"), A("r16"), ACT.Abs, bias=col(5))
    ts(A("rs1"), A("r16"), 0.5, -2 * BIG, ALU.is_gt, ALU.mult)
    ts(A("rst16"), A("rs1"), BIG, None, ALU.add)
    cp(A("ulist"), A("ilist"))
    ts(A("nm2"), A("nm1"), 0.5, 2 * BIG, ALU.is_gt, ALU.mult)
    ts(A("nm16"), A("nm2"), -BIG, None, ALU.add)
    act(A("rz16"), A("r16"), ACT.Sign)
    act(A("ioj"), A("ij"), ACT.Copy, scale=1.0 / 512)
    act(A("srt0", C, POS), A("eone", 0, POS - C), ACT.Copy, scale=0.75)
    quant("u", 0, 128, A("ut"))
    ul = A("ulist")
    qa, qb, sa, sb = A("qua"), A("qu"), A("sua"), A("su")
    op(V, lambda e: e.tensor_copy(qa[0].bitcast(dt.uint32), qb[0].bitcast(dt.uint32).indirect(ul[0])), [qa[1]], [qb[1], ul[1]])
    op(V, lambda e: e.tensor_copy(sa[0], sb[0].indirect(ul[0])), [sa[1]], [sb[1], ul[1]])
    for i in range(6):
        ms(A("mt%d" % i, 4 * (336 - 64 * i), 4 * MTN[i]), 0.0)
    ms(A("rsum", 0, 1), 0.0)
    ms(A("wsc", 0, 8), 0.0)
    ms(A("xw0", 1536, 2048), 0.0)
    ts(A("c24"), A("ct"), col(1), None, ALU.add)
    ts(A("si"), A("st"), col(1), None, ALU.add)
    ts(A("hm1"), A("hm"), col(4), 8.0 - 1.0e6, ALU.is_equal, ALU.mult)
    ts(A("msk", 0, 32), A("hm1"), 1.0e6, None, ALU.add)
    ms(A("msk", 32, 33), 8.0)
    ts(A("rc", 1, 2), col(1), 3.5, 1.0e6, ALU.is_gt, ALU.mult)
    ts(A("rc", 0, 1), A("rc", 1, 2), col(1), 8.0 * 54, ALU.add, ALU.add)

    def scalar_constants():
        act(A("n41"), A("r4"), ACT.Abs, bias=col(6))
        act(A("n42"), A("n41"), ACT.Sign, bias=-0.5)
        act(A("nm4"), A("n42"), ACT.Copy, scale=BIG)
        act(A("rs4"), A("r4"), ACT.Sign, bias=-0.5)
        act(A("rst4"), A("rs4"), ACT.Copy, scale=-BIG)
        act(A("ni"), A("ij"), ACT.Identity, scale=1.0 / 512, bias=NB0 / 512.0)
        act(A("ebth"), A("ebt"), ACT.Copy, scale=0.5)

    cores = list(T.cores)
    n = len(cores)
    peers = [cores[(rank + k) % n] for k in range(1, n)]
    E = topo.engines(core, peers[0])
    quads = [E[0::4], E[2::4], E[1::4], E[3::4]]
    order = sorted(peers, key=lambda c: topo.die(c) == topo.die(core))
    codes_of = {order[0]: 0, order[1]: 1, order[2]: 2}
    plane_of = {order[0]: 3, order[1]: 2, order[2]: 0}
    bits = lambda k: sum(1 << e for e in quads[k])

    def send(src, base, dst, back, rsem, lsem):
        need(G, [], [A("q" + src)[1], A("s" + src)[1]])
        for kind, table in (("q", codes_of), ("s", plane_of)):
            tr = []
            for k in range(1, n):
                c = cores[(rank - k) % n] if back else cores[(rank + k) % n]
                lo = base + P * (k - 1)
                a = T[kind + src][:, lo:lo + P]
                b = T[kind + dst][:, P * (k - 1):P * k]
                if kind == "q":
                    a, b = a.bitcast(dt.uint8), b.bitcast(dt.uint8)
                rid, pid, _ = topo.addr(c)
                tr.append(RemoteDMATransfer(dst_ids=[DstId(rid=rid, pnc=pid)], dma_engine_mask=bits(table[c]), remote_sem=T.sem[rsem], src=a, dst=b))
            g.remote_dma_fused(tr, local_sem=T.sem[lsem])

    def arrived(dst, sem):
        note([A("q" + dst)[1], A("s" + dst)[1]], [], (sem, 8 * (n - 1), "far"))

    ps = lambda b, m: A("ps%d" % b, 0, m)
    slots = {}
    for i, t in enumerate([None] + list(range(23, 0, -1))):
        slots[t] = (i // 4, i % 4)
    jk = [0]
    for t in range(1, 24):
        jk.append(jk[-1] + 16 * t)

    def one_round(r):
        xw, srt, last = "xw%d" % r, "srt%d" % r, r == 1
        quant("x%d" % r, 0, C, A(xw, 0, 4 * C))
        mm(0, C, "ua", 0, "x%d" % r, 0)
        mm(1, C, "u", 0, "x%d" % r, 0)
        tt(A("vm"), ps(0, C), A("nm16"), ALU.max)
        act(A("rl"), ps(1, C), ACT.Relu)
        act(A("fb"), A("rl"), ACT.Sign)
        scan(A("zz"), A("rst16"), A("vm"), ALU.max, ALU.min)
        tt(A("mt0", 0, 4 * C, 4), ps(0, C), A("zz"), ALU.is_gt)
        for t in range(23, 0, -1):
            i, f = slots[t]
            w = 16 * t
            m = A("mt%d" % i, f, 4 * w, 4)
            ts(m, ps(0, w), A("zz", w + 15, w + 16), None, ALU.is_ge)
            act(A("jk", jk[t - 1], jk[t - 1] + w), m, ACT.Copy, acc=A("rsum", t, t + 1))
            if f == 3:
                if r == 0 and i == 0:
                    quant("g", 0, 128, A("gt"))
                quant("m%d" % i, 0, MTN[i], A("mt%d" % i))
                mm(2, MTN[i], "g", 0, "m%d" % i, 0, i == 0, i == 5)
            if t == 12:
                tt(A("fj"), A("fb"), A("ioj"), ALU.add)
                scan(A("dg"), A("rz16"), A("mt0", 0, 4 * C, 4), ALU.mult, ALU.add)
                tt(A("cd"), A("c24"), A("dg", 15, C, 16), ALU.add)
        if r == 0:
            scalar_constants()
        tt(A("cx"), ps(2, C), A("nm16"), ALU.max)
        scan(A("z2"), A("rst16"), A("cx"), ALU.max, ALU.min)
        tt(A("pd"), A("cd"), A("z2", 15, C, 16), ALU.subtract)
        tt(A("pf"), A("pd"), A("rsum"), ALU.add)
        cp(A("pl"), A("pf"))
        put(A(srt, 0, C), A("pl"), A("fj"))
        ts(A("fs"), A(srt, 0, C), 1.0, 1.0, ALU.is_ge, ALU.add)
        scan(A("wsc", 8, 8 + C), A("fs"), A("fs"), ALU.add, ALU.max)
        tot = A("wsc", 7 + C, 8 + C)
        thr, rem = tot, A("rc", 0, 1)
        for m, (mult, lo, hi, nxt) in enumerate(((4.0, 54, 154, 119), (3.0, 119, 271, 207), (2.0, 207, 348, None))):
            ts(A("cm", 0, hi - lo), A("wsc", 7 + lo, 7 + hi), mult, thr, ALU.mult, ALU.is_lt)
            c, k = A("cnt", m, m + 1), A("kk", m, m + 1)
            red(c, A("cm", 0, hi - lo), ALU.add)
            ts(A("ky", 0, 33), A("msk", 0, 33), c, rem, ALU.mult, ALU.add)
            kt, ky = A("kt"), A("ky", 0, 32)
            op(V, lambda e: e.transpose(kt[0], ky[0]), [kt[1]], [ky[1]])
            red(k, kt, ALU.min)
            of = A("of", 2 * m, 2 * m + 1)
            ts(of, k, 0.125, 7.0, ALU.mult, ALU.add)
            if nxt is not None:
                wa = A("wa", 16 * m, 16 * m + 16)
                pick(V, wa, A("wsc", 0, 392), of)
                ts(A("rm", m, m + 1), A("ky", 32, 33), k, 1.0e6, ALU.is_equal, ALU.mult)
                ts(A("rr", m, m + 1), A("rm", m, m + 1), rem, 8.0 * (nxt - lo), ALU.add, ALU.add)
                rem = A("rr", m, m + 1)
                ts(A("th", m, m + 1), A("wa", 16 * m, 16 * m + 1), mult - 2.0, tot, ALU.mult, ALU.add)
                thr = A("th", m, m + 1)
        tmp = lambda k: A("tmp", 24 * k, 24 * k + 24)
        c1 = lambda b, k: A(b, k, k + 1)
        ts(A("aa", 0, 3), A("of", 0, 6, 2), -7.0, None, ALU.add)
        ts(A("a8", 0, 3), A("aa", 0, 3), -8.0, None, ALU.mult)
        ts(A("am", 0, 3), A("aa", 0, 3), -float(C), None, ALU.add)
        tt(A("w3", 0, 3), A("a8", 0, 3), A("kk", 0, 3), ALU.add)
        red(A("w4", 0, 1), A("w3", 0, 3), ALU.add)
        ts(tmp(3), A("ki"), c1("w3", 1), c1("aa", 0), ALU.is_equal, ALU.mult)
        ts(A("w4", 1, 2), A("w4", 0, 1), -1.0, 6.0, ALU.mult, ALU.add)
        ts(tmp(4), A("ki"), c1("w3", 2), c1("aa", 1), ALU.is_equal, ALU.mult)
        tt(tmp(7), A("si"), tmp(3), ALU.add)
        ts(tmp(5), A("ki"), c1("w4", 1), c1("aa", 2), ALU.is_equal, ALU.mult)
        ts(tmp(0), A("ki"), c1("w3", 0), c1("am", 0), ALU.is_equal, ALU.mult)
        ts(tmp(1), A("ki"), c1("w3", 1), c1("am", 1), ALU.is_equal, ALU.mult)
        tt(tmp(8), tmp(4), tmp(5), ALU.add)
        ts(tmp(2), A("ki"), c1("w3", 2), c1("am", 2), ALU.is_equal, ALU.mult)
        tt(tmp(6), tmp(0), tmp(1), ALU.add)
        tt(tmp(10), tmp(7), tmp(8), ALU.add)
        tt(tmp(9), tmp(6), tmp(2), ALU.add)
        tt(tmp(11), tmp(10), tmp(9), ALU.is_ge)
        tt(tmp(12), tmp(11), A("koff"), ALU.mult)
        tt(tmp(13), tmp(10), tmp(12), ALU.add)
        ts(A("pu"), tmp(13), float(C), None, ALU.add)
        picktt(A("gm"), A(srt), A("pu"), A("nm4"), ALU.max)
        scan(A("zs"), A("rst4"), A("gm"), ALU.max, ALU.min)
        ts(A("l1"), A("zs", 3, C, 4), 2048.0, col(2), ALU.mult, ALU.add)
        win = A(xw, 0, 3584)
        pick(V, A("bt", 0, 768), win, A("l1", 0, 48))
        pick(S, A("bt", 768, 1536), win, A("l1", 48, 96))
        quant("b%d" % r, 0, C, A("bt"))
        send("b%d" % r, P, "lb%d" % r, False, "ab%d" % r, "lb%d" % r)
        arrived("lb%d" % r, "ab%d" % r)
        if r == 0:
            quant("eh", 0, 512, A("ebth"))
        for b in range(4):
            mm(4 + b, 128, "eh", 128 * b, "b%d" % r, 0)
        tt(A("ge"), A(srt, 0, P), A("nm4", 0, P), ALU.max)
        scan(A("ze"), A("rst4", 0, P), A("ge"), ALU.max, ALU.min)
        ts(A("l3"), A("ze", 3, P, 4), 2048.0, col(2), ALU.mult, ALU.add)
        pick(S, A("e3", 0, 384), win, A("l3"), scale=0.5)
        act(A("e3", 384, 768), A("e3", 0, 384), ACT.Copy)
        act(A("e3", 768, 1152), A("e3", 0, 384), ACT.Copy)
        if r == 0:
            quant("e1", 0, 512, A("ebt"))
        for b in range(4):
            tt(A("zt0", b, 384, 4), ps(4 + b, P), A("e3", b, 384, 4), ALU.add)
        quant("z0", 0, 128, A("zt0"))
        for b in range(4):
            mm(b, 128, "w", 128 * b, "z0", 0)
        for b in range(4):
            act(A("ht0", b, 384, 4), ps(b, P), ACT.Copy, scale=0.03125)
        put(A(srt), A("pu"), A("ni"))
        for c in range(2):
            for b in range(4):
                mm(b + 4 - 4 * c, HALF, "eh", 128 * b, "lb%d" % r, HALF * c)
        for c in range(2):
            lo, hi = 4 * HALF * c, 4 * HALF * (c + 1)
            for b in range(4):
                tt(A("zt", lo + b, hi, 4), ps(b + 4 - 4 * c, HALF), A("e3", lo + b, hi, 4), ALU.add)
            quant("z", HALF * c, HALF * (c + 1), A("zt", lo, hi))
            for b in (0, 2, 1, 3):
                mm(b + 4 - 4 * c, HALF, "w", 128 * b, "z", HALF * c)
        for c in range(2):
            lo, hi = 4 * HALF * c, 4 * HALF * (c + 1)
            for b in range(2):
                ts(A("ht", lo + b, hi, 4), ps(b + 4 - 4 * c, HALF), 0.03125, None, ALU.mult)
            for b in range(2, 4):
                act(A("ht", lo + b, hi, 4), ps(b + 4 - 4 * c, HALF), ACT.Copy, scale=0.03125)
        quant("h%d" % r, 0, R3, A("ht"))
        send("h%d" % r, 0, "lh%d" % r, True, "ah%d" % r, "lh%d" % r)
        arrived("lh%d" % r, "ah%d" % r)
        quant("h0k", 0, 128, A("ht0"))
        for b in range(4):
            mm(4 + b, 128, "e1", 128 * b, "h0k", 0)
        picktt(A("gm2"), A(srt, 0, C), A("pl"), A("nm4"), ALU.max)
        scan(A("zs2"), A("rst4"), A("gm2"), ALU.max, ALU.min)
        ts(A("l2"), A("zs2", 3, C, 4), 2048.0, col(2), ALU.mult, ALU.add)
        base = 4 * NB0
        for b in range(4):
            tt(A(xw, base + b, base + 384, 4), ps(4 + b, P), A("bt", b, 384, 4), ALU.add)
        if last:
            pick(S, A("slg"), A(srt, 0, C), A("pl"))
            act(A("sl1"), A("slg"), ACT.Relu, scale=512.0, bias=1.0 - NB0)
            act(A("sl2"), A("sl1"), ACT.Identity, bias=-1.0)
            buf, at = HOME["sl2"]
            dma(SY, T.sl[:], T[buf][0:128:16, at:at + C], [], [A("sl2")[1]])
        else:
            act(A("srt1", C, POS), A("eone", 0, POS - C), ACT.Copy, scale=0.75)
            quant("v", 0, 128, A("vt"))
        for b in range(4):
            mm(4 + b, R3, "e1", 128 * b, "lh%d" % r, 0)
        for b in range(4):
            tt(A(xw, base + 384 + b, base + 1536, 4), ps(4 + b, R3), A("bt", 384 + b, 1536, 4), ALU.add)
        xn = "xf" if last else "xw1"
        full = A(xw, 0, 4 * XW)
        pick(V, A(xn, 0, 768), full, A("l2", 0, 48))
        pick(S, A(xn, 768, 1536), full, A("l2", 48, 96))
        if not last:
            a, b = A(xn, 2048, 2048 + 4 * C), A(xn, 0, 4 * C)
            dma(SY, a[0], b[0], [a[1]], [b[1]])

    one_round(0)
    one_round(1)

    h = C // 2
    quant("xf", 0, C, A("xf"))
    mm(3, h, "v", 0, "xf", 0)
    mm(2, h, "v", 0, "xf", h)
    qf = A("qxf")
    dma(SY, T.oc[:], qf[0].bitcast(dt.uint8), [], [qf[1]])
    for k in range(4):
        dma(SY, T.osc[4 * k:4 * k + 4, :], T["sxf"][32 * k:32 * k + 4, :], [], [A("sxf")[1]])
    y0, y1 = A("yt", 0, h), A("yt", h, C)
    cp(y0, ps(3, h))
    act(y1, ps(2, h), ACT.Copy)
    dma(SY, T.y[:, 0:h], y0[0], [], [y0[1]])
    dma(S, T.y[:, h:C], y1[0], [], [y1[1]])
    for q in (V, S, PE, G):
        g.sync.wait_ge(T.sem["s" + q], count[q])
    for s in used:
        g.sync.wait_ge(T.sem[s], 16)
    for r in range(2):
        g.wait_ge(T.sem["lb%d" % r], 8 * (n - 1))
        g.wait_ge(T.sem["lh%d" % r], 8 * (n - 1))
